import numpy as np
import ml_dtypes


def mxq(x, axis, fmt="e4m3"):
    dtype, down = {"e4m3": (ml_dtypes.float8_e4m3fn, 7), "e5m2": (ml_dtypes.float8_e5m2, 14)}[fmt]
    v = np.moveaxis(np.asarray(x, np.float32).astype(ml_dtypes.bfloat16).astype(np.float64), axis, -1)
    blocks = v.reshape(v.shape[:-1] + (-1, 32))
    amax = np.abs(blocks).max(-1, keepdims=True)
    byte = np.maximum(np.where(amax > 0, np.frexp(amax)[1] - 1 + 127, 0) - down, 1)
    scale = np.exp2(byte - 127.0)
    codes = (blocks / scale).astype(np.float32).astype(dtype).astype(np.float64)
    return np.moveaxis((codes * scale).reshape(v.shape), -1, axis)


WIDE = False


def mx_kscale(k):
    if not WIDE:
        return np.ones(k)
    levels = np.array([10, -10, 5, -5, 0])
    if k % 512:
        return np.exp2(np.random.permutation(np.resize(levels, k // 32))).repeat(32)
    a = np.empty((k // 512, 16))
    for p in range(k // 512):
        a[p, :8] = np.random.permutation(np.resize(levels, 8))
        for g in range(8):
            far = levels[np.abs(levels - a[p, g]) >= 10]
            a[p, g + 8] = far[np.random.randint(len(far))]
    return np.exp2(a.ravel()).repeat(32)


def f64(x):
    return np.asarray(x).astype(np.float64)


def striped(idx):
    return np.tile(idx.reshape(-1, 16).T, (8, 1)).astype(np.uint16)


def unstriped(offs):
    return offs[:16].T.reshape(-1).astype(np.int64)


E2M1 = np.array([0.0, 0.5, 1.0, 1.5, 2.0, 3.0, 4.0, 6.0, -0.0, -0.5, -1.0, -1.5, -2.0, -3.0, -4.0, -6.0])


def pack_weight(w, fmt):
    k, n = w.shape
    w = f64(np.asarray(w, np.float32).astype(ml_dtypes.bfloat16)).reshape(k // 32, 32, n)
    amax = np.abs(w).max(1)
    if fmt == "e4m3":
        byte = np.frexp(amax)[1] - 1 + 127 - 7
    else:
        mant, ex = np.frexp(amax / 6.0)
        byte = np.where(mant > 0.5, ex, ex - 1) + 127
    byte = np.clip(np.where(amax > 0, byte, 1), 1, 254)
    scaled = (w * np.exp2(127.0 - byte)[:, None, :]).reshape(k, n).astype(np.float32)
    by_word = np.ascontiguousarray(scaled.reshape(k // 512, 128, 4, n).transpose(0, 1, 3, 2))
    if fmt == "e4m3":
        words = by_word.astype(ml_dtypes.float8_e4m3fn).view(np.uint8)
    else:
        c = by_word.astype(ml_dtypes.float4_e2m1fn).view(np.uint8) & 0xF
        words = (c[..., 0::2] | (c[..., 1::2] << 4)).reshape(k // 512, 128, 2 * n)
    return np.ascontiguousarray(words), np.ascontiguousarray(byte.astype(np.uint8).reshape(k // 512, 16, n))


def unpack_weight(words, scales, fmt):
    g, _, n = scales.shape
    words = np.ascontiguousarray(words).reshape(g, 128, n, -1)
    if fmt == "e4m3":
        vals = words.view(ml_dtypes.float8_e4m3fn).astype(np.float64)
    else:
        nib = np.empty((g, 128, n, 4), np.uint8)
        nib[..., 0::2] = words & 0xF
        nib[..., 1::2] = words >> 4
        vals = E2M1[nib]
    vals = vals * np.repeat(np.exp2(scales.astype(np.float64) - 127.0), 8, axis=1)[..., None]
    return vals.transpose(0, 1, 3, 2).reshape(g * 512, n)


def gelu(v):
    return 0.5 * v * (1.0 + np.tanh(np.sqrt(2.0 / np.pi) * (v + 0.044715 * v**3)))


K, H, T, S, T3, S2, T2, P = 1536, 1024, 2048, 512, 2048, 512, 1024, 512

def setup_inputs():
    n = np.random.standard_normal
    s = mx_kscale(K)[:, None]
    u = mx_kscale(H)[:, None]
    tab_words, tab_scales = pack_weight(n((K, T)) * s, "e4m3")
    tab2_words, tab2_scales = pack_weight(n((H, T3)) / np.sqrt(H) / u, "e4m3")
    w2_words, w2_scales = pack_weight(0.8 * n((K, H)) / np.sqrt(K) / s * u.T, "e2m1")
    return {
        "tab_words": tab_words, "tab_scales": tab_scales,
        "tab2_words": tab2_words, "tab2_scales": tab2_scales,
        "w1": (1.5 * n((K, H)) / np.sqrt(K) / s).astype(np.float32),
        "w2_words": w2_words, "w2_scales": w2_scales,
        "w3": (0.9 * n((K, S2)) / np.sqrt(K) / s).astype(np.float32),
        "gain": (np.exp(0.3 * n(H)) * u[:, 0]).astype(np.float32),
        "page0": (n((H, T2)) * u).astype(np.float32),
        "wgs": np.exp(0.3 * n((128, S))).astype(np.float32),
        "trail": np.exp(0.3 * n(S2)).astype(np.float32),
        "offs": striped(np.random.permutation(T)[:S]),
        "offs2": striped(np.random.permutation(T3)[:S2]),
        "offs3": striped(np.random.permutation(T2)[:S]),
        "pos1": striped(np.random.permutation(T2)[:P]),
        "pos2": striped(np.random.permutation(T2)[:P]),
    }

def reference(tab_words, tab_scales, tab2_words, tab2_scales, w1, w2_words, w2_scales, w3, gain, page0, wgs, trail, offs, offs2, offs3, pos1, pos2):
    v = unpack_weight(tab_words, tab_scales, "e4m3")[:, unstriped(offs)]
    v2 = unpack_weight(tab2_words, tab2_scales, "e4m3")[:, unstriped(offs2)]
    w2 = unpack_weight(w2_words, w2_scales, "e2m1")
    a1 = mxq(f64(w1), 0, "e4m3").T @ v
    act = 0.5 * a1 * (1.0 + np.tanh(np.sqrt(2.0 / np.pi) * (a1 + 0.044715 * a1 ** 3)))
    h = f64(gain)[:, None] * act + (w2.T @ v)
    page = f64(page0).copy()
    page[:, unstriped(offs3)] = np.tile(f64(wgs), (H // 128, 1)) * h
    e = v2.T @ mxq(page, 0, "e4m3")
    d = mxq(f64(w3), 0, "e4m3").T @ v
    lead = e[:, unstriped(pos1)] + d
    return np.maximum(lead, f64(trail)[:, None] * e[:, unstriped(pos2)])

@@ -1,0 +1,303 @@
+from contextlib import ExitStack
+
+import concourse.mybir as mybir
+
+K, H, T, S, T2 = 1536, 1024, 2048, 512, 1024
+FLOPS = 5100273664
+
+F32 = mybir.dt.float32
+BF16 = mybir.dt.bfloat16
+I32 = mybir.dt.int32
+U32 = mybir.dt.uint32
+U16 = mybir.dt.uint16
+U8 = mybir.dt.uint8
+FP8X4 = mybir.dt.float8_e4m3fn_x4
+FP4X4 = mybir.dt.float4_e2m1fn_x4
+ALU = mybir.AluOpType
+ACT = mybir.ActivationFunctionType
+
+P = 128
+PACK = 4
+KP = P * PACK
+NA = K // KP
+NB = H // KP
+NM = S // P
+AL = 64
+
+
+def tile_list_ore_ejection_scores_kernel(
+    tc, tab_words, tab_scales, tab2_words, tab2_scales, w1, w2_words, w2_scales, w3,
+    gain, page0, wgs, trail, offs, offs2, offs3, pos1, pos2, out,
+):
+    nc = tc.nc
+    with ExitStack() as ctx:
+        lists = ctx.enter_context(tc.tile_pool(name="lists", bufs=1))
+        sb = ctx.enter_context(tc.tile_pool(name="sb", bufs=1))
+        hp = ctx.enter_context(tc.tile_pool(name="hp", bufs=1))
+        ps = ctx.enter_context(tc.psum_pool(name="ps", bufs=1))
+
+        def sbuf(name, shape, dtype, tag=None, bufs=1):
+            return sb.tile(shape, dtype, name=name, tag=tag or name, bufs=bufs, align_bytes=AL)
+
+        def placed(name, shape, dtype, kib):
+            return hp.tile(shape, dtype, name=name, tag=name, align_bytes=AL, offset=int(kib * 1024))
+
+        def load_list(name, dram):
+            t = lists.tile([P, S // 16], U16, name=name)
+            nc.sync.dma_start(t[:], dram)
+            return t
+
+        def zero_planes(name, width):
+            t = sbuf(name, [P, width], U8)
+            nc.vector.memset(t[:].bitcast(I32), 0)
+            return t
+
+        def load_planes(queue, t, dram, passes):
+            src = dram.rearrange("a (q r) c -> r q a c", r=4)
+            for r in range(4):
+                queue.dma_start(
+                    out=t[r:P:32, :].bitcast(I32).rearrange("q (a w) -> q a w", a=passes),
+                    in_=src[r].bitcast(I32),
+                )
+
+        def load_words(name, dram_pass):
+            t = sbuf(name, [P, T], I32, tag="tabw", bufs=3)
+            nc.sync.dma_start(out=t[:], in_=dram_pass.rearrange("p t i -> p (t i)").bitcast(I32))
+            return t
+
+        def load_raw(name, w, a, c0, tag="raw", bufs=3):
+            t = sbuf(name, [P, PACK, KP], F32, tag=tag, bufs=bufs)
+            nc.sync.dma_start(
+                out=t[:], in_=w[a * KP:(a + 1) * KP, c0:c0 + KP].rearrange("(p j) c -> p j c", j=PACK)
+            )
+            return t
+
+        def load_page(s):
+            b, t = divmod(s, PACK)
+            pg = sbuf("page%d" % s, [P, T2], F32)
+            rows = page0[b * KP:(b + 1) * KP, :].rearrange("(p t) n -> t p n", t=PACK)
+            nc.sync.dma_start(out=pg[:], in_=rows[t])
+            return pg
+
+        def load_wgs(t):
+            wt = sbuf("wgs%d" % t, [P, S], F32)
+            rows = wgs.rearrange("(q t) j -> t q j", t=PACK)
+            nc.sync.dma_start(out=wt[:], in_=rows[t].partition_broadcast(4))
+            return wt
+
+        def gather(dst, window, offsets):
+            nc.vector.tensor_copy(dst, window.indirect(offsets[:]))
+
+        def quantise(name, grouped, width):
+            codes = sbuf(name + "c", [P, width], U32)
+            scales = sbuf(name + "s", [P, width], U8)
+            nc.vector.quantize_mx(out=codes[:].bitcast(FP8X4), scales=scales[:], in_=grouped)
+            return codes, scales
+
+        def quantise_w1(name, raw, t0, nt, kib):
+            g = placed(name + "g", [P, nt * P * PACK], BF16, kib)
+            nc.scalar.copy(
+                out=g[:].rearrange("p (t m j) -> p m t j", t=nt, j=PACK),
+                in_=raw[:].rearrange("p j (m t) -> p m t j", t=PACK)[:, :, t0:t0 + nt, :],
+            )
+            codes, scales = quantise(name, g[:], nt * P)
+            return [(codes[:, i * P:(i + 1) * P], scales[:, i * P:(i + 1) * P]) for i in range(nt)]
+
+        def quantise_w3(name, raw, kib):
+            g = placed(name + "g", [P, KP * PACK], BF16, kib)
+            nc.scalar.copy(
+                out=g[:].rearrange("p (c i j) -> p c j i", i=4, j=PACK),
+                in_=raw[:].rearrange("p j (c i) -> p c j i", i=4),
+            )
+            return quantise(name, g[:], KP)
+
+        def mx(acc, lhs, lhs_scale, rhs, rhs_scale, first, last, lhs_dtype=FP8X4):
+            nc.tensor.matmul_mx(
+                out=acc, lhsT=lhs.bitcast(lhs_dtype), lhsT_scale=lhs_scale,
+                rhs=rhs.bitcast(FP8X4), rhs_scale=rhs_scale, start=first, stop=last,
+            )
+
+        tabs = zero_planes("tabs", NA * T)
+        w2s = zero_planes("w2s", NA * H)
+        tab2s = zero_planes("tab2s", T)
+        vw, vs = [], []
+        w1q = {}
+        w2d, w2sd = {}, {}
+
+        def deal(name, src, dtype):
+            dst = sbuf(name, [P, NA * KP], dtype)
+            nc.vector.tensor_copy(dst[:].rearrange("p (a t q) -> p t a q", a=NA, t=PACK), src)
+            return dst
+
+        def head_loads(a):
+            return load_words("tabw%d" % a, tab_words[a]), load_raw("w1r0%d" % a, w1, a, 0)
+
+        def head_pass(a, words, raw):
+            g = placed("vw%d" % a, [P, S], U32, (28, 16, 20)[a])
+            gather(g[:], words[:].bitcast(U32), offs_t)
+            vw.append(g)
+            gs = sbuf("vs%d" % a, [P, S], U8)
+            gather(gs[:], tabs[:, a * T:(a + 1) * T], offs_t)
+            vs.append(gs)
+            if a < NA - 1:
+                w1q[0, a] = quantise_w1("w1q0%d" % a, raw, 0, 4, 16 + 4 * a)
+            else:
+                w1q[0, a] = (
+                    quantise_w1("w1q02x", raw, 0, 1, 18)
+                    + quantise_w1("w1q02y", raw, 1, 1, 19)
+                    + quantise_w1("w1q02z", raw, 2, 2, 22)
+                )
+
+        offs_t = load_list("offs", offs)
+        first_words = load_words("tabw0", tab_words[0])
+        offs3_t = load_list("offs3", offs3)
+        gain_t = sbuf("gain", [P, NB * PACK], F32)
+        nc.sync.dma_start(
+            out=gain_t[:].rearrange("p (b t) -> p b t", t=PACK),
+            in_=gain.rearrange("(b p t) -> p b t", b=NB, t=PACK),
+        )
+        w2w = sbuf("w2w", [P, NA * H], U16)
+        nc.sync.dma_start(
+            out=w2w[:].bitcast(I32).rearrange("p (a w) -> p a w", a=NA),
+            in_=w2_words.rearrange("a p c -> p a c").bitcast(I32),
+        )
+        load_planes(nc.sync, tabs, tab_scales, NA)
+        first_raw = load_raw("w1r00", w1, 0, 0)
+        load_planes(nc.sync, w2s, w2_scales, NA)
+        head_pass(0, first_words, first_raw)
+
+        def deal_w2(b):
+            for name, src, dtype, into in (("w2d", w2w, U16, w2d), ("w2sd", w2s, U8, w2sd)):
+                half = src[:].rearrange("p (a b q t) -> p b t a q", a=NA, b=NB, t=PACK)[:, b]
+                into[b] = deal("%s%d" % (name, b), half, dtype)
+
+        deal_w2(0)
+        head_pass(1, *head_loads(1))
+        head_pass(2, *head_loads(2))
+        deal_w2(1)
+
+        pages, wgs_t = {}, {}
+
+        def feature_slice(s):
+            b, t = divmod(s, PACK)
+            a1 = ps.tile([P, S], F32, name="a1_%d" % s, tag="a1", bufs=3)
+            for a in range(NA):
+                codes, scales = w1q[b, a][t]
+                mx(a1[:], codes, scales, vw[a][:], vs[a][:], a == 0, a == NA - 1)
+            lin = ps.tile([P, S], F32, name="lin_%d" % s, tag="lin", bufs=2)
+            for a in range(NA):
+                cols = slice(a * KP + t * P, a * KP + (t + 1) * P)
+                mx(lin[:], w2d[b][:, cols], w2sd[b][:, cols], vw[a][:], vs[a][:], a == 0, a == NA - 1, FP4X4)
+            if s < 2:
+                act = placed("act%d" % s, [P, S], F32, (11, 5)[s])
+            else:
+                act = sbuf("act%d" % s, [P, S], F32, tag="act", bufs=3)
+            nc.scalar.activation(out=act[:], in_=a1[:], func=ACT.Gelu_apprx_tanh)
+            h = placed("h%d" % s, [P, S], F32, (1, 0, 2, 3, 2, 4, 2, 4)[s])
+            nc.vector.scalar_tensor_tensor(
+                out=h[:], in0=act[:], scalar=gain_t[:, s:s + 1], in1=lin[:], op0=ALU.mult, op1=ALU.add
+            )
+            nc.vector.tensor_tensor(pages[s][:].indirect(offs3_t[:]), h[:], wgs_t[t][:], ALU.mult)
+
+        wgs_t[0] = load_wgs(0)
+        pages[0] = load_page(0)
+        raws = []
+        for a in range(NA):
+            if a < NA - 1:
+                raws.append(load_raw("w1r1%d" % a, w1, a, KP))
+            else:
+                raws.append(load_raw("w1r1%d" % a, w1, a, KP, tag="rawlast", bufs=1))
+            wgs_t[a + 1] = load_wgs(a + 1)
+            pages[a + 1] = load_page(a + 1)
+        feature_slice(0)
+        w1q[1, 0] = quantise_w1("w1q10", raws[0], 0, 4, 8)
+        feature_slice(1)
+        w1q[1, 1] = quantise_w1("w1q11", raws[1], 0, 4, 12)
+        feature_slice(2)
+        w1q[1, 2] = quantise_w1("w1q12x", raws[2], 0, 2, 6) + quantise_w1("w1q12y", raws[2], 2, 2, 4)
+        feature_slice(3)
+
+        w3r = []
+        pages[4] = load_page(4)
+        w3r.append(load_raw("w3r0", w3, 0, 0))
+        pages[5] = load_page(5)
+        pages[6] = load_page(6)
+        w3r.append(load_raw("w3r1", w3, 1, 0))
+        pages[7] = load_page(7)
+        w3r.append(load_raw("w3r2", w3, 2, 0))
+        offs2_t = load_list("offs2", offs2)
+        tab2w = [load_words("tab2w%d" % a, tab2_words[a]) for a in range(NB)]
+        for q in range(4):
+            nc.sync.dma_start(
+                out=tab2s[32 * q:32 * q + 4 * NB, :].bitcast(I32),
+                in_=tab2_scales[:, 4 * q:4 * q + 4, :].bitcast(I32),
+            )
+        pos1_t = load_list("pos1", pos1)
+        pos2_t = load_list("pos2", pos2)
+        trail_t = sbuf("trail", [P, NM], F32)
+        with nc.allow_non_contiguous_dma(reason="one value a partition"):
+            nc.sync.dma_start(out=trail_t[:], in_=trail.rearrange("(c p) -> p c", p=P))
+
+        def round_page(flat, s, cols):
+            nc.scalar.copy(out=flat[:, s % PACK, cols], in_=pages[s][:, cols])
+
+        def weave(engine_copy, name, flat, cols, width):
+            g = sbuf(name, [P, width * PACK], BF16)
+            engine_copy(
+                g[:].rearrange("p (c i t) -> p c t i", i=4, t=PACK),
+                flat[:, :, cols].rearrange("p t (c i) -> p c t i", i=4),
+            )
+            return g
+
+        whole = slice(0, T2)
+        halves = [slice(0, S), slice(S, T2)]
+        feature_slice(4)
+        feature_slice(5)
+        flat0 = sbuf("flat0", [P, PACK, T2], BF16, tag="rawlast")
+        for s in range(PACK):
+            round_page(flat0, s, whole)
+        w3q = [quantise_w3("w3q0", w3r[0], 8)]
+        feature_slice(6)
+        feature_slice(7)
+        g0 = weave(nc.scalar.copy, "pg0", flat0, whole, T2)
+        pc0, psc0 = quantise("pq0", g0[:], T2)
+        w3q.append(quantise_w3("w3q1", w3r[1], 12))
+        w3q.append(quantise_w3("w3q2", w3r[2], 24))
+        flat1 = sbuf("flat1", [P, PACK, T2], BF16)
+        for s in range(PACK, 2 * PACK - 1):
+            round_page(flat1, s, whole)
+
+        v2s = placed("v2s", [P, S], U8, 4)
+        gather(v2s[:], tab2s[:], offs2_t)
+        v2w = [placed("v2w0", [P, S], U32, 2), placed("v2w1", [P, S], U32, 4.5)]
+        for a in range(NB):
+            gather(v2w[a][:], tab2w[a][:].bitcast(U32), offs2_t)
+
+        pq1 = []
+        for i, cols in enumerate(halves):
+            round_page(flat1, 2 * PACK - 1, cols)
+            g = weave(nc.scalar.copy, "pg1%d" % i, flat1, cols, S)
+            pq1.append(quantise("pq1%d" % i, g[:], S))
+
+        for m in range(NM):
+            cols = slice(m * P, (m + 1) * P)
+            e = sbuf("e%d" % m, [P, T2], F32, tag="raw", bufs=3)
+            for i, half in enumerate(halves):
+                acc = ps.tile([P, S], F32, name="e%d_%d" % (m, i), tag="e", bufs=3)
+                mx(acc[:], v2w[0][:, cols], v2s[:, cols], pc0[:, half], psc0[:, half], True, False)
+                mx(acc[:], v2w[1][:, cols], v2s[4:P, cols], pq1[i][0][:], pq1[i][1][:], False, True)
+                nc.scalar.copy(out=e[:, half], in_=acc[:])
+            acc = ps.tile([P, S], F32, name="d%d" % m, tag="lin", bufs=2)
+            for a in range(NA):
+                mx(acc[:], w3q[a][0][:, cols], w3q[a][1][:, cols], vw[a][:], vs[a][:], a == 0, a == NA - 1)
+            direct = sbuf("direct%d" % m, [P, S], F32, tag="direct", bufs=2)
+            nc.scalar.copy(out=direct[:], in_=acc[:])
+            back = sbuf("back%d" % m, [P, S], F32, tag="act", bufs=3)
+            gather(back[:], e[:], pos2_t)
+            lead = sbuf("lead%d" % m, [P, S], F32, tag="lead", bufs=2)
+            nc.vector.tensor_tensor(lead[:], e[:].indirect(pos1_t[:]), direct[:], ALU.add)
+            res = sbuf("res%d" % m, [P, S], F32, tag="res", bufs=2)
+            nc.vector.scalar_tensor_tensor(
+                out=res[:], in0=back[:], scalar=trail_t[:, m:m + 1], in1=lead[:], op0=ALU.mult, op1=ALU.max
+            )
+            nc.sync.dma_start(out=out[cols, :], in_=res[:])

@@ -47,8 +47,8 @@ def tile_list_ore_ejection_scores_kernel(
             nc.sync.dma_start(t[:], dram)
             return t
 
-        def zero_planes(name, width):
-            t = sbuf(name, [P, width], U8)
+        def zero_planes(name, width, kib):
+            t = placed(name, [P, width], U8, kib)
             nc.vector.memset(t[:].bitcast(I32), 0)
             return t
 
@@ -65,8 +65,11 @@ def tile_list_ore_ejection_scores_kernel(
             nc.sync.dma_start(out=t[:], in_=dram_pass.rearrange("p t i -> p (t i)").bitcast(I32))
             return t
 
-        def load_raw(name, w, a, c0, tag="raw", bufs=3):
-            t = sbuf(name, [P, PACK, KP], F32, tag=tag, bufs=bufs)
+        def load_raw(name, w, a, c0, kib=None):
+            if kib is None:
+                t = sbuf(name, [P, PACK, KP], F32, tag="raw", bufs=3)
+            else:
+                t = placed(name, [P, PACK, KP], F32, kib)
             nc.sync.dma_start(
                 out=t[:], in_=w[a * KP:(a + 1) * KP, c0:c0 + KP].rearrange("(p j) c -> p j c", j=PACK)
             )
@@ -79,11 +82,12 @@ def tile_list_ore_ejection_scores_kernel(
             nc.sync.dma_start(out=pg[:], in_=rows[t])
             return pg
 
-        def load_wgs(t):
-            wt = sbuf("wgs%d" % t, [P, S], F32)
-            rows = wgs.rearrange("(q t) j -> t q j", t=PACK)
-            nc.sync.dma_start(out=wt[:], in_=rows[t].partition_broadcast(4))
-            return wt
+        def load_wgs(name, t0, nt):
+            wt = sbuf(name, [P, nt, S], F32)
+            rows = wgs.rearrange("(q t) j -> q t j", t=PACK)[:, t0:t0 + nt, :]
+            for u in range(4):
+                nc.sync.dma_start(out=wt[32 * u:32 * (u + 1)], in_=rows)
+            return [wt[:, i, :] for i in range(nt)]
 
         def gather(dst, window, offsets):
             nc.vector.tensor_copy(dst, window.indirect(offsets[:]))
@@ -117,9 +121,13 @@ def tile_list_ore_ejection_scores_kernel(
                 rhs=rhs.bitcast(FP8X4), rhs_scale=rhs_scale, start=first, stop=last,
             )
 
-        tabs = zero_planes("tabs", NA * T)
-        w2s = zero_planes("w2s", NA * H)
-        tab2s = zero_planes("tab2s", T)
+        tabs = zero_planes("tabs", NA * T, 30)
+        w2s = zero_planes("w2s", NA * H, 42)
+        tab2s = zero_planes("tab2s", T, 62)
+        warm_in = sbuf("warm_in", [P, 1], F32)
+        nc.gpsimd.memset(warm_in[:], 0.0)
+        warm_out = sbuf("warm_out", [P, 1], F32)
+        nc.scalar.activation(out=warm_out[:], in_=warm_in[:], func=ACT.Gelu_apprx_tanh)
         vw, vs = [], []
         w1q = {}
         w2d, w2sd = {}, {}
@@ -156,7 +164,7 @@ def tile_list_ore_ejection_scores_kernel(
             out=gain_t[:].rearrange("p (b t) -> p b t", t=PACK),
             in_=gain.rearrange("(b p t) -> p b t", b=NB, t=PACK),
         )
-        w2w = sbuf("w2w", [P, NA * H], U16)
+        w2w = placed("w2w", [P, NA * H], U16, 36)
         nc.sync.dma_start(
             out=w2w[:].bitcast(I32).rearrange("p (a w) -> p a w", a=NA),
             in_=w2_words.rearrange("a p c -> p a c").bitcast(I32),
@@ -176,7 +184,7 @@ def tile_list_ore_ejection_scores_kernel(
         head_pass(2, *head_loads(2))
         deal_w2(1)
 
-        pages, wgs_t = {}, {}
+        pages, wgs_t = {}, []
 
         def feature_slice(s):
             b, t = divmod(s, PACK)
@@ -197,17 +205,18 @@ def tile_list_ore_ejection_scores_kernel(
             nc.vector.scalar_tensor_tensor(
                 out=h[:], in0=act[:], scalar=gain_t[:, s:s + 1], in1=lin[:], op0=ALU.mult, op1=ALU.add
             )
-            nc.vector.tensor_tensor(pages[s][:].indirect(offs3_t[:]), h[:], wgs_t[t][:], ALU.mult)
+            nc.vector.tensor_tensor(pages[s][:].indirect(offs3_t[:]), h[:], wgs_t[t], ALU.mult)
 
-        wgs_t[0] = load_wgs(0)
+        wgs_t.extend(load_wgs("wgs0", 0, 1))
         pages[0] = load_page(0)
         raws = []
         for a in range(NA):
             if a < NA - 1:
                 raws.append(load_raw("w1r1%d" % a, w1, a, KP))
             else:
-                raws.append(load_raw("w1r1%d" % a, w1, a, KP, tag="rawlast", bufs=1))
-            wgs_t[a + 1] = load_wgs(a + 1)
+                raws.append(load_raw("w1r1%d" % a, w1, a, KP, 46))
+            if a == 0:
+                wgs_t.extend(load_wgs("wgs1", 1, 3))
             pages[a + 1] = load_page(a + 1)
         feature_slice(0)
         w1q[1, 0] = quantise_w1("w1q10", raws[0], 0, 4, 8)
@@ -253,9 +262,10 @@ def tile_list_ore_ejection_scores_kernel(
         halves = [slice(0, S), slice(S, T2)]
         feature_slice(4)
         feature_slice(5)
-        flat0 = sbuf("flat0", [P, PACK, T2], BF16, tag="rawlast")
-        for s in range(PACK):
-            round_page(flat0, s, whole)
+        flat0 = placed("flat0", [P, PACK, T2], F32, 30)
+        flat1 = placed("flat1", [P, PACK, T2], F32, 46)
+        for s in range(6):
+            nc.gpsimd.dma_start(out=(flat0, flat1)[s // PACK][:, s % PACK, :], in_=pages[s][:])
         w3q = [quantise_w3("w3q0", w3r[0], 8)]
         feature_slice(6)
         feature_slice(7)
@@ -263,9 +273,7 @@ def tile_list_ore_ejection_scores_kernel(
         pc0, psc0 = quantise("pq0", g0[:], T2)
         w3q.append(quantise_w3("w3q1", w3r[1], 12))
         w3q.append(quantise_w3("w3q2", w3r[2], 24))
-        flat1 = sbuf("flat1", [P, PACK, T2], BF16)
-        for s in range(PACK, 2 * PACK - 1):
-            round_page(flat1, s, whole)
+        round_page(flat1, 6, whole)
 
         v2s = placed("v2s", [P, S], U8, 4)
         gather(v2s[:], tab2s[:], offs2_t)

@@ -1,6 +1,7 @@
 from contextlib import ExitStack
 
 import concourse.mybir as mybir
+from concourse.masks import make_identity
 
 K, H, T, S, T2 = 1536, 1024, 2048, 512, 1024
 FLOPS = 5100273664
@@ -82,12 +83,27 @@ def tile_list_ore_ejection_scores_kernel(
             nc.sync.dma_start(out=pg[:], in_=rows[t])
             return pg
 
-        def load_wgs(name, t0, nt):
-            wt = sbuf(name, [P, nt, S], F32)
-            rows = wgs.rearrange("(q t) j -> q t j", t=PACK)[:, t0:t0 + nt, :]
-            for u in range(4):
-                nc.sync.dma_start(out=wt[32 * u:32 * (u + 1)], in_=rows)
-            return [wt[:, i, :] for i in range(nt)]
+        def deal_wgs(rows):
+            ident = sbuf("ident", [P, P], F32)
+            make_identity(nc, ident[:])
+            turned = ps.tile([P, PACK, P], F32, name="turned", tag="e", bufs=3)
+            for c in range(PACK):
+                nc.tensor.transpose(turned[:, c, :], rows[:, c * P:(c + 1) * P], ident[:])
+            spread = placed("spread", [P, PACK, PACK, 4, 32], F32, 54)
+            for c in range(PACK):
+                src = turned[:, c, :].rearrange("p (q t) -> p t q", t=PACK).unsqueeze(2)
+                nc.scalar.copy(out=spread[:, c], in_=src.to_broadcast([P, PACK, 4, 32]))
+            dealt = []
+            for t in range(PACK):
+                back = ps.tile([P, S], F32, name="wgsb%d" % t, tag="e", bufs=3)
+                for c in range(PACK):
+                    nc.tensor.transpose(
+                        back[:, c * P:(c + 1) * P], spread[:, c, t].rearrange("p u q -> p (u q)"), ident[:]
+                    )
+                wt = sbuf("wgs%d" % t, [P, S], F32)
+                nc.scalar.copy(out=wt[:], in_=back[:])
+                dealt.append(wt[:])
+            return dealt
 
         def gather(dst, window, offsets):
             nc.vector.tensor_copy(dst, window.indirect(offsets[:]))
@@ -138,10 +154,15 @@ def tile_list_ore_ejection_scores_kernel(
             return dst
 
         def head_loads(a):
-            return load_words("tabw%d" % a, tab_words[a]), load_raw("w1r0%d" % a, w1, a, 0)
+            if a < NA - 1:
+                return load_words("tabw%d" % a, tab_words[a]), load_raw("w1r0%d" % a, w1, a, 0)
+            raw = load_raw("w1r0%d" % a, w1, a, 0)
+            return load_words("tabw%d" % a, tab_words[a]), raw
 
         def head_pass(a, words, raw):
-            g = placed("vw%d" % a, [P, S], U32, (28, 16, 20)[a])
+            if a == NA - 1:
+                w1q[0, a] = quantise_w1("w1q02x", raw, 0, 2, 18)
+            g = placed("vw%d" % a, [P, S], U32, (28, 16, 18)[a])
             gather(g[:], words[:].bitcast(U32), offs_t)
             vw.append(g)
             gs = sbuf("vs%d" % a, [P, S], U8)
@@ -150,15 +171,13 @@ def tile_list_ore_ejection_scores_kernel(
             if a < NA - 1:
                 w1q[0, a] = quantise_w1("w1q0%d" % a, raw, 0, 4, 16 + 4 * a)
             else:
-                w1q[0, a] = (
-                    quantise_w1("w1q02x", raw, 0, 1, 18)
-                    + quantise_w1("w1q02y", raw, 1, 1, 19)
-                    + quantise_w1("w1q02z", raw, 2, 2, 22)
-                )
+                w1q[0, a] += quantise_w1("w1q02y", raw, 2, 2, 22)
 
         offs_t = load_list("offs", offs)
         first_words = load_words("tabw0", tab_words[0])
-        offs3_t = load_list("offs3", offs3)
+        wgs_rows = placed("wgs_rows", [P, S], F32, 24)
+        nc.sync.dma_start(out=wgs_rows[:], in_=wgs)
+        wgs_t = deal_wgs(wgs_rows)
         gain_t = sbuf("gain", [P, NB * PACK], F32)
         nc.sync.dma_start(
             out=gain_t[:].rearrange("p (b t) -> p b t", t=PACK),
@@ -184,7 +203,8 @@ def tile_list_ore_ejection_scores_kernel(
         head_pass(2, *head_loads(2))
         deal_w2(1)
 
-        pages, wgs_t = {}, []
+        pages = {}
+        act_at = {0: 11, 1: 5, 3: 8, 4: 12, 5: 24}
 
         def feature_slice(s):
             b, t = divmod(s, PACK)
@@ -196,8 +216,8 @@ def tile_list_ore_ejection_scores_kernel(
             for a in range(NA):
                 cols = slice(a * KP + t * P, a * KP + (t + 1) * P)
                 mx(lin[:], w2d[b][:, cols], w2sd[b][:, cols], vw[a][:], vs[a][:], a == 0, a == NA - 1, FP4X4)
-            if s < 2:
-                act = placed("act%d" % s, [P, S], F32, (11, 5)[s])
+            if s in act_at:
+                act = placed("act%d" % s, [P, S], F32, act_at[s])
             else:
                 act = sbuf("act%d" % s, [P, S], F32, tag="act", bufs=3)
             nc.scalar.activation(out=act[:], in_=a1[:], func=ACT.Gelu_apprx_tanh)
@@ -207,7 +227,7 @@ def tile_list_ore_ejection_scores_kernel(
             )
             nc.vector.tensor_tensor(pages[s][:].indirect(offs3_t[:]), h[:], wgs_t[t], ALU.mult)
 
-        wgs_t.extend(load_wgs("wgs0", 0, 1))
+        offs3_t = load_list("offs3", offs3)
         pages[0] = load_page(0)
         raws = []
         for a in range(NA):
@@ -215,8 +235,6 @@ def tile_list_ore_ejection_scores_kernel(
                 raws.append(load_raw("w1r1%d" % a, w1, a, KP))
             else:
                 raws.append(load_raw("w1r1%d" % a, w1, a, KP, 46))
-            if a == 0:
-                wgs_t.extend(load_wgs("wgs1", 1, 3))
             pages[a + 1] = load_page(a + 1)
         feature_slice(0)
         w1q[1, 0] = quantise_w1("w1q10", raws[0], 0, 4, 8)
@@ -262,17 +280,18 @@ def tile_list_ore_ejection_scores_kernel(
         halves = [slice(0, S), slice(S, T2)]
         feature_slice(4)
         feature_slice(5)
-        flat0 = placed("flat0", [P, PACK, T2], F32, 30)
-        flat1 = placed("flat1", [P, PACK, T2], F32, 46)
-        for s in range(6):
+        flat0 = placed("flat0", [P, PACK, T2], F32, 46)
+        flat1 = placed("flat1", [P, PACK, T2], F32, 30)
+        for s in range(5):
             nc.gpsimd.dma_start(out=(flat0, flat1)[s // PACK][:, s % PACK, :], in_=pages[s][:])
-        w3q = [quantise_w3("w3q0", w3r[0], 8)]
         feature_slice(6)
         feature_slice(7)
+        w3q = [quantise_w3("w3q0", w3r[0], 8)]
         g0 = weave(nc.scalar.copy, "pg0", flat0, whole, T2)
         pc0, psc0 = quantise("pq0", g0[:], T2)
         w3q.append(quantise_w3("w3q1", w3r[1], 12))
         w3q.append(quantise_w3("w3q2", w3r[2], 24))
+        round_page(flat1, 5, whole)
         round_page(flat1, 6, whole)
 
         v2s = placed("v2s", [P, S], U8, 4)

@@ -23,7 +23,23 @@ KP = P * PACK
 NA = K // KP
 NB = H // KP
 NM = S // P
-AL = 64
+QUADS = 4
+RUN = 4
+ALIGN = 64
+
+PLACE = {
+    "h0": 1, "h1": 0, "h2": 2, "h3": 3, "h4": 2, "h5": 4, "h6": 2, "h7": 4,
+    "v2w0": 2, "v2s": 4, "v2w1": 4.5,
+    "act0": 11, "act1": 5, "w1q10g": 8, "w1q11g": 12, "w1q12xg": 6, "w1q12yg": 4,
+    "w3q0g": 8, "w3q1g": 12, "w3q2g": 24,
+    "w1q00g": 16, "w1q01g": 20, "w1q02xg": 18, "w1q02yg": 22, "vw0": 28, "vw1": 16, "vw2": 18,
+    "tabs": 30, "w2w0": 36, "w2w1": 39, "w2s": 42, "flat1": 30,
+    "w1r12": 46, "flat0": 46,
+    "wgs_rows": 24, "spread": 54, "tab2s": 62,
+    "w1r00": 94, "wgs0": 94, "wgs1": 96, "wgs2": 98, "wgs3": 100,
+    "tabw0": 64, "tabw1": 72, "tabw2": 80, "tab2w0": 64, "tab2w1": 72,
+    "w2d1": 80, "w2sd1": 84, "w2d0": 88, "w2sd0": 91,
+}
 
 
 def tile_list_ore_ejection_scores_kernel(
@@ -38,71 +54,71 @@ def tile_list_ore_ejection_scores_kernel(
         ps = ctx.enter_context(tc.psum_pool(name="ps", bufs=1))
 
         def sbuf(name, shape, dtype, tag=None, bufs=1):
-            return sb.tile(shape, dtype, name=name, tag=tag or name, bufs=bufs, align_bytes=AL)
+            if name in PLACE:
+                offset = int(PLACE[name] * 1024)
+                return hp.tile(shape, dtype, name=name, tag=name, align_bytes=ALIGN, offset=offset)
+            return sb.tile(shape, dtype, name=name, tag=tag or name, bufs=bufs, align_bytes=ALIGN)
 
-        def placed(name, shape, dtype, kib):
-            return hp.tile(shape, dtype, name=name, tag=name, align_bytes=AL, offset=int(kib * 1024))
+        def bank(name, shape, tag):
+            return ps.tile(shape, F32, name=name, tag=tag, bufs={"a1": 3, "lin": 2, "e": 3}[tag])
 
         def load_list(name, dram):
-            t = lists.tile([P, S // 16], U16, name=name)
-            nc.sync.dma_start(t[:], dram)
-            return t
+            offsets = lists.tile([P, S // 16], U16, name=name)
+            nc.sync.dma_start(offsets[:], dram)
+            return offsets
 
-        def zero_planes(name, width, kib):
-            t = placed(name, [P, width], U8, kib)
-            nc.vector.memset(t[:].bitcast(I32), 0)
-            return t
+        def zeroed_scale_tile(name, width):
+            rows = sbuf(name, [P, width], U8)
+            nc.vector.memset(rows[:].bitcast(I32), 0)
+            return rows
 
-        def load_planes(queue, t, dram, passes):
+        def load_scale_rows(rows, dram):
             src = dram.rearrange("a (q r) c -> r q a c", r=4)
             for r in range(4):
-                queue.dma_start(
-                    out=t[r:P:32, :].bitcast(I32).rearrange("q (a w) -> q a w", a=passes),
+                nc.sync.dma_start(
+                    out=rows[r:P:32, :].bitcast(I32).rearrange("q (a w) -> q a w", a=NA),
                     in_=src[r].bitcast(I32),
                 )
 
         def load_words(name, dram_pass):
-            t = sbuf(name, [P, T], I32, tag="tabw", bufs=3)
-            nc.sync.dma_start(out=t[:], in_=dram_pass.rearrange("p t i -> p (t i)").bitcast(I32))
-            return t
+            words = sbuf(name, [P, T], I32)
+            nc.sync.dma_start(out=words[:], in_=dram_pass.rearrange("p t i -> p (t i)").bitcast(I32))
+            return words
 
-        def load_raw(name, w, a, c0, kib=None):
-            if kib is None:
-                t = sbuf(name, [P, PACK, KP], F32, tag="raw", bufs=3)
-            else:
-                t = placed(name, [P, PACK, KP], F32, kib)
+        def load_raw(name, w, a, c0):
+            raw = sbuf(name, [P, PACK, KP], F32, tag="raw", bufs=NA)
             nc.sync.dma_start(
-                out=t[:], in_=w[a * KP:(a + 1) * KP, c0:c0 + KP].rearrange("(p j) c -> p j c", j=PACK)
+                out=raw[:], in_=w[a * KP:(a + 1) * KP, c0:c0 + KP].rearrange("(p j) c -> p j c", j=PACK)
             )
-            return t
+            return raw
 
         def load_page(s):
             b, t = divmod(s, PACK)
-            pg = sbuf("page%d" % s, [P, T2], F32)
+            page = sbuf("page%d" % s, [P, T2], F32)
             rows = page0[b * KP:(b + 1) * KP, :].rearrange("(p t) n -> t p n", t=PACK)
-            nc.sync.dma_start(out=pg[:], in_=rows[t])
-            return pg
+            nc.sync.dma_start(out=page[:], in_=rows[t])
+            return page
 
         def deal_wgs(rows):
             ident = sbuf("ident", [P, P], F32)
             make_identity(nc, ident[:])
-            turned = ps.tile([P, PACK, P], F32, name="turned", tag="e", bufs=3)
+            turned = bank("turned", [P, PACK, P], "e")
             for c in range(PACK):
                 nc.tensor.transpose(turned[:, c, :], rows[:, c * P:(c + 1) * P], ident[:])
-            spread = placed("spread", [P, PACK, PACK, 4, 32], F32, 54)
+            spread = sbuf("spread", [P, PACK, PACK, QUADS, 32], F32)
             for c in range(PACK):
                 src = turned[:, c, :].rearrange("p (q t) -> p t q", t=PACK).unsqueeze(2)
-                nc.scalar.copy(out=spread[:, c], in_=src.to_broadcast([P, PACK, 4, 32]))
+                nc.scalar.copy(out=spread[:, c], in_=src.to_broadcast([P, PACK, QUADS, 32]))
             dealt = []
             for t in range(PACK):
-                back = ps.tile([P, S], F32, name="wgsb%d" % t, tag="e", bufs=3)
+                returned = bank("wgsb%d" % t, [P, S], "e")
                 for c in range(PACK):
                     nc.tensor.transpose(
-                        back[:, c * P:(c + 1) * P], spread[:, c, t].rearrange("p u q -> p (u q)"), ident[:]
+                        returned[:, c * P:(c + 1) * P], spread[:, c, t].rearrange("p u q -> p (u q)"), ident[:]
                     )
-                wt = sbuf("wgs%d" % t, [P, S], F32)
-                nc.scalar.copy(out=wt[:], in_=back[:])
-                dealt.append(wt[:])
+                weights = sbuf("wgs%d" % t, [P, S], F32)
+                nc.scalar.copy(out=weights[:], in_=returned[:])
+                dealt.append(weights[:])
             return dealt
 
         def gather(dst, window, offsets):
@@ -114,22 +130,22 @@ def tile_list_ore_ejection_scores_kernel(
             nc.vector.quantize_mx(out=codes[:].bitcast(FP8X4), scales=scales[:], in_=grouped)
             return codes, scales
 
-        def quantise_w1(name, raw, t0, nt, kib):
-            g = placed(name + "g", [P, nt * P * PACK], BF16, kib)
+        def quantise_w1(name, raw, t0, nt):
+            grouped = sbuf(name + "g", [P, nt * P * PACK], BF16)
             nc.scalar.copy(
-                out=g[:].rearrange("p (t m j) -> p m t j", t=nt, j=PACK),
+                out=grouped[:].rearrange("p (t m j) -> p m t j", t=nt, j=PACK),
                 in_=raw[:].rearrange("p j (m t) -> p m t j", t=PACK)[:, :, t0:t0 + nt, :],
             )
-            codes, scales = quantise(name, g[:], nt * P)
+            codes, scales = quantise(name, grouped[:], nt * P)
             return [(codes[:, i * P:(i + 1) * P], scales[:, i * P:(i + 1) * P]) for i in range(nt)]
 
-        def quantise_w3(name, raw, kib):
-            g = placed(name + "g", [P, KP * PACK], BF16, kib)
+        def quantise_w3(name, raw):
+            grouped = sbuf(name + "g", [P, KP * PACK], BF16)
             nc.scalar.copy(
-                out=g[:].rearrange("p (c i j) -> p c j i", i=4, j=PACK),
-                in_=raw[:].rearrange("p j (c i) -> p c j i", i=4),
+                out=grouped[:].rearrange("p (c i j) -> p c j i", i=RUN, j=PACK),
+                in_=raw[:].rearrange("p j (c i) -> p c j i", i=RUN),
             )
-            return quantise(name, g[:], KP)
+            return quantise(name, grouped[:], KP)
 
         def mx(acc, lhs, lhs_scale, rhs, rhs_scale, first, last, lhs_dtype=FP8X4):
             nc.tensor.matmul_mx(
@@ -137,91 +153,87 @@ def tile_list_ore_ejection_scores_kernel(
                 rhs=rhs.bitcast(FP8X4), rhs_scale=rhs_scale, start=first, stop=last,
             )
 
-        tabs = zero_planes("tabs", NA * T, 30)
-        w2s = zero_planes("w2s", NA * H, 42)
-        tab2s = zero_planes("tab2s", T, 62)
+        tabs = zeroed_scale_tile("tabs", NA * T)
+        w2s = zeroed_scale_tile("w2s", NA * H)
+        tab2s = zeroed_scale_tile("tab2s", T)
         warm_in = sbuf("warm_in", [P, 1], F32)
         nc.gpsimd.memset(warm_in[:], 0.0)
         warm_out = sbuf("warm_out", [P, 1], F32)
         nc.scalar.activation(out=warm_out[:], in_=warm_in[:], func=ACT.Gelu_apprx_tanh)
+
         vw, vs = [], []
         w1q = {}
         w2d, w2sd = {}, {}
 
         def deal(name, src, dtype):
             dst = sbuf(name, [P, NA * KP], dtype)
-            nc.vector.tensor_copy(dst[:].rearrange("p (a t q) -> p t a q", a=NA, t=PACK), src)
+            nc.vector.tensor_copy(dst[:].rearrange("p (a t m) -> p t a m", a=NA, t=PACK), src)
             return dst
 
-        def head_loads(a):
-            if a < NA - 1:
-                return load_words("tabw%d" % a, tab_words[a]), load_raw("w1r0%d" % a, w1, a, 0)
-            raw = load_raw("w1r0%d" % a, w1, a, 0)
-            return load_words("tabw%d" % a, tab_words[a]), raw
+        def w2_words_half(b):
+            words = sbuf("w2w%d" % b, [P, NA * KP], U16)
+            nc.sync.dma_start(
+                out=words[:].bitcast(I32).rearrange("p (a w) -> p a w", a=NA),
+                in_=w2_words[:, :, 2 * b * KP:2 * (b + 1) * KP].rearrange("a p c -> p a c").bitcast(I32),
+            )
+            w2d[b] = deal("w2d%d" % b, words[:].rearrange("p (a m t) -> p t a m", a=NA, t=PACK), U16)
 
-        def head_pass(a, words, raw):
-            if a == NA - 1:
-                w1q[0, a] = quantise_w1("w1q02x", raw, 0, 2, 18)
-            g = placed("vw%d" % a, [P, S], U32, (28, 16, 18)[a])
-            gather(g[:], words[:].bitcast(U32), offs_t)
-            vw.append(g)
-            gs = sbuf("vs%d" % a, [P, S], U8)
-            gather(gs[:], tabs[:, a * T:(a + 1) * T], offs_t)
-            vs.append(gs)
-            if a < NA - 1:
-                w1q[0, a] = quantise_w1("w1q0%d" % a, raw, 0, 4, 16 + 4 * a)
-            else:
-                w1q[0, a] += quantise_w1("w1q02y", raw, 2, 2, 22)
+        def w2_scales_half(b):
+            half = w2s[:].rearrange("p (a b m t) -> p b t a m", a=NA, b=NB, t=PACK)[:, b]
+            w2sd[b] = deal("w2sd%d" % b, half, U8)
 
+        def gather_tab(a, words):
+            picked = sbuf("vw%d" % a, [P, S], U32)
+            gather(picked[:], words[:].bitcast(U32), offs_t)
+            vw.append(picked)
+            picked_scales = sbuf("vs%d" % a, [P, S], U8)
+            gather(picked_scales[:], tabs[:, a * T:(a + 1) * T], offs_t)
+            vs.append(picked_scales)
+
+        words0 = load_words("tabw0", tab_words[0])
         offs_t = load_list("offs", offs)
-        first_words = load_words("tabw0", tab_words[0])
-        wgs_rows = placed("wgs_rows", [P, S], F32, 24)
+        wgs_rows = sbuf("wgs_rows", [P, S], F32)
         nc.sync.dma_start(out=wgs_rows[:], in_=wgs)
+        raw0 = load_raw("w1r00", w1, 0, 0)
+        w2_words_half(0)
+        load_scale_rows(tabs, tab_scales)
+        gather_tab(0, words0)
+        w1q[0, 0] = quantise_w1("w1q00", raw0, 0, PACK)
         wgs_t = deal_wgs(wgs_rows)
+        words1 = load_words("tabw1", tab_words[1])
+        raw1 = load_raw("w1r01", w1, 1, 0)
+        load_scale_rows(w2s, w2_scales)
+        w2_scales_half(0)
+        gather_tab(1, words1)
+        w1q[0, 1] = quantise_w1("w1q01", raw1, 0, PACK)
+        raw2 = load_raw("w1r02", w1, 2, 0)
+        words2 = load_words("tabw2", tab_words[2])
+        w1q[0, 2] = quantise_w1("w1q02x", raw2, 0, 2)
+        gather_tab(2, words2)
+        w1q[0, 2] += quantise_w1("w1q02y", raw2, 2, 2)
         gain_t = sbuf("gain", [P, NB * PACK], F32)
         nc.sync.dma_start(
             out=gain_t[:].rearrange("p (b t) -> p b t", t=PACK),
             in_=gain.rearrange("(b p t) -> p b t", b=NB, t=PACK),
         )
-        w2w = placed("w2w", [P, NA * H], U16, 36)
-        nc.sync.dma_start(
-            out=w2w[:].bitcast(I32).rearrange("p (a w) -> p a w", a=NA),
-            in_=w2_words.rearrange("a p c -> p a c").bitcast(I32),
-        )
-        load_planes(nc.sync, tabs, tab_scales, NA)
-        first_raw = load_raw("w1r00", w1, 0, 0)
-        load_planes(nc.sync, w2s, w2_scales, NA)
-        head_pass(0, first_words, first_raw)
-
-        def deal_w2(b):
-            for name, src, dtype, into in (("w2d", w2w, U16, w2d), ("w2sd", w2s, U8, w2sd)):
-                half = src[:].rearrange("p (a b q t) -> p b t a q", a=NA, b=NB, t=PACK)[:, b]
-                into[b] = deal("%s%d" % (name, b), half, dtype)
-
-        deal_w2(0)
-        head_pass(1, *head_loads(1))
-        head_pass(2, *head_loads(2))
-        deal_w2(1)
+        w2_scales_half(1)
+        w2_words_half(1)
 
         pages = {}
-        act_at = {0: 11, 1: 5, 3: 8, 4: 12, 5: 24}
 
         def feature_slice(s):
             b, t = divmod(s, PACK)
-            a1 = ps.tile([P, S], F32, name="a1_%d" % s, tag="a1", bufs=3)
+            a1 = bank("a1_%d" % s, [P, S], "a1")
             for a in range(NA):
                 codes, scales = w1q[b, a][t]
                 mx(a1[:], codes, scales, vw[a][:], vs[a][:], a == 0, a == NA - 1)
-            lin = ps.tile([P, S], F32, name="lin_%d" % s, tag="lin", bufs=2)
+            lin = bank("lin_%d" % s, [P, S], "lin")
             for a in range(NA):
                 cols = slice(a * KP + t * P, a * KP + (t + 1) * P)
                 mx(lin[:], w2d[b][:, cols], w2sd[b][:, cols], vw[a][:], vs[a][:], a == 0, a == NA - 1, FP4X4)
-            if s in act_at:
-                act = placed("act%d" % s, [P, S], F32, act_at[s])
-            else:
-                act = sbuf("act%d" % s, [P, S], F32, tag="act", bufs=3)
+            act = sbuf("act%d" % s, [P, S], F32, tag="act", bufs=3)
             nc.scalar.activation(out=act[:], in_=a1[:], func=ACT.Gelu_apprx_tanh)
-            h = placed("h%d" % s, [P, S], F32, (1, 0, 2, 3, 2, 4, 2, 4)[s])
+            h = sbuf("h%d" % s, [P, S], F32)
             nc.vector.scalar_tensor_tensor(
                 out=h[:], in0=act[:], scalar=gain_t[:, s:s + 1], in1=lin[:], op0=ALU.mult, op1=ALU.add
             )
@@ -231,17 +243,14 @@ def tile_list_ore_ejection_scores_kernel(
         pages[0] = load_page(0)
         raws = []
         for a in range(NA):
-            if a < NA - 1:
-                raws.append(load_raw("w1r1%d" % a, w1, a, KP))
-            else:
-                raws.append(load_raw("w1r1%d" % a, w1, a, KP, 46))
+            raws.append(load_raw("w1r1%d" % a, w1, a, KP))
             pages[a + 1] = load_page(a + 1)
         feature_slice(0)
-        w1q[1, 0] = quantise_w1("w1q10", raws[0], 0, 4, 8)
+        w1q[1, 0] = quantise_w1("w1q10", raws[0], 0, PACK)
         feature_slice(1)
-        w1q[1, 1] = quantise_w1("w1q11", raws[1], 0, 4, 12)
+        w1q[1, 1] = quantise_w1("w1q11", raws[1], 0, PACK)
         feature_slice(2)
-        w1q[1, 2] = quantise_w1("w1q12x", raws[2], 0, 2, 6) + quantise_w1("w1q12y", raws[2], 2, 2, 4)
+        w1q[1, 2] = quantise_w1("w1q12x", raws[2], 0, 2) + quantise_w1("w1q12y", raws[2], 2, 2)
         feature_slice(3)
 
         w3r = []
@@ -253,8 +262,8 @@ def tile_list_ore_ejection_scores_kernel(
         pages[7] = load_page(7)
         w3r.append(load_raw("w3r2", w3, 2, 0))
         offs2_t = load_list("offs2", offs2)
-        tab2w = [load_words("tab2w%d" % a, tab2_words[a]) for a in range(NB)]
-        for q in range(4):
+        tab2w = [load_words("tab2w%d" % b, tab2_words[b]) for b in range(NB)]
+        for q in range(QUADS):
             nc.sync.dma_start(
                 out=tab2s[32 * q:32 * q + 4 * NB, :].bitcast(I32),
                 in_=tab2_scales[:, 4 * q:4 * q + 4, :].bitcast(I32),
@@ -268,55 +277,53 @@ def tile_list_ore_ejection_scores_kernel(
         def round_page(flat, s, cols):
             nc.scalar.copy(out=flat[:, s % PACK, cols], in_=pages[s][:, cols])
 
-        def weave(engine_copy, name, flat, cols, width):
-            g = sbuf(name, [P, width * PACK], BF16)
-            engine_copy(
-                g[:].rearrange("p (c i t) -> p c t i", i=4, t=PACK),
-                flat[:, :, cols].rearrange("p t (c i) -> p c t i", i=4),
+        def weave_and_quantise(b, i, flat):
+            grouped = sbuf("pg%d%d" % (b, i), [P, S * PACK], BF16)
+            nc.scalar.copy(
+                out=grouped[:].rearrange("p (c i t) -> p c t i", i=RUN, t=PACK),
+                in_=flat[:, :, halves[i]].rearrange("p t (c i) -> p c t i", i=RUN),
             )
-            return g
+            return quantise("pq%d%d" % (b, i), grouped[:], S)
 
         whole = slice(0, T2)
         halves = [slice(0, S), slice(S, T2)]
         feature_slice(4)
         feature_slice(5)
-        flat0 = placed("flat0", [P, PACK, T2], F32, 46)
-        flat1 = placed("flat1", [P, PACK, T2], F32, 30)
-        for s in range(5):
-            nc.gpsimd.dma_start(out=(flat0, flat1)[s // PACK][:, s % PACK, :], in_=pages[s][:])
         feature_slice(6)
+        flat0 = sbuf("flat0", [P, PACK, T2], BF16)
+        for s in range(PACK):
+            round_page(flat0, s, whole)
         feature_slice(7)
-        w3q = [quantise_w3("w3q0", w3r[0], 8)]
-        g0 = weave(nc.scalar.copy, "pg0", flat0, whole, T2)
-        pc0, psc0 = quantise("pq0", g0[:], T2)
-        w3q.append(quantise_w3("w3q1", w3r[1], 12))
-        w3q.append(quantise_w3("w3q2", w3r[2], 24))
-        round_page(flat1, 5, whole)
-        round_page(flat1, 6, whole)
+        w3q = [quantise_w3("w3q0", w3r[0])]
+        pq0 = [weave_and_quantise(0, i, flat0) for i in range(len(halves))]
+        w3q.append(quantise_w3("w3q1", w3r[1]))
+        w3q.append(quantise_w3("w3q2", w3r[2]))
+        flat1 = sbuf("flat1", [P, PACK, T2], BF16)
+        last = NB * PACK - 1
+        for s in range(PACK, last):
+            round_page(flat1, s, whole)
 
-        v2s = placed("v2s", [P, S], U8, 4)
+        v2s = sbuf("v2s", [P, S], U8)
         gather(v2s[:], tab2s[:], offs2_t)
-        v2w = [placed("v2w0", [P, S], U32, 2), placed("v2w1", [P, S], U32, 4.5)]
-        for a in range(NB):
-            gather(v2w[a][:], tab2w[a][:].bitcast(U32), offs2_t)
-
+        v2w = [sbuf("v2w%d" % b, [P, S], U32) for b in range(NB)]
+        for b in range(NB):
+            gather(v2w[b][:], tab2w[b][:].bitcast(U32), offs2_t)
         pq1 = []
-        for i, cols in enumerate(halves):
-            round_page(flat1, 2 * PACK - 1, cols)
-            g = weave(nc.scalar.copy, "pg1%d" % i, flat1, cols, S)
-            pq1.append(quantise("pq1%d" % i, g[:], S))
+        for i, half in enumerate(halves):
+            round_page(flat1, last, half)
+            pq1.append(weave_and_quantise(1, i, flat1))
 
         for m in range(NM):
-            cols = slice(m * P, (m + 1) * P)
-            e = sbuf("e%d" % m, [P, T2], F32, tag="raw", bufs=3)
+            rows = slice(m * P, (m + 1) * P)
+            e = sbuf("e%d" % m, [P, T2], F32, tag="raw", bufs=NA)
             for i, half in enumerate(halves):
-                acc = ps.tile([P, S], F32, name="e%d_%d" % (m, i), tag="e", bufs=3)
-                mx(acc[:], v2w[0][:, cols], v2s[:, cols], pc0[:, half], psc0[:, half], True, False)
-                mx(acc[:], v2w[1][:, cols], v2s[4:P, cols], pq1[i][0][:], pq1[i][1][:], False, True)
+                acc = bank("e%d_%d" % (m, i), [P, S], "e")
+                mx(acc[:], v2w[0][:, rows], v2s[:, rows], pq0[i][0][:], pq0[i][1][:], True, False)
+                mx(acc[:], v2w[1][:, rows], v2s[4:P, rows], pq1[i][0][:], pq1[i][1][:], False, True)
                 nc.scalar.copy(out=e[:, half], in_=acc[:])
-            acc = ps.tile([P, S], F32, name="d%d" % m, tag="lin", bufs=2)
+            acc = bank("d%d" % m, [P, S], "lin")
             for a in range(NA):
-                mx(acc[:], w3q[a][0][:, cols], w3q[a][1][:, cols], vw[a][:], vs[a][:], a == 0, a == NA - 1)
+                mx(acc[:], w3q[a][0][:, rows], w3q[a][1][:, rows], vw[a][:], vs[a][:], a == 0, a == NA - 1)
             direct = sbuf("direct%d" % m, [P, S], F32, tag="direct", bufs=2)
             nc.scalar.copy(out=direct[:], in_=acc[:])
             back = sbuf("back%d" % m, [P, S], F32, tag="act", bufs=3)
@@ -327,4 +334,4 @@ def tile_list_ore_ejection_scores_kernel(
             nc.vector.scalar_tensor_tensor(
                 out=res[:], in0=back[:], scalar=trail_t[:, m:m + 1], in1=lead[:], op0=ALU.mult, op1=ALU.max
             )
-            nc.sync.dma_start(out=out[cols, :], in_=res[:])
+            nc.sync.dma_start(out=out[rows, :], in_=res[:])

from contextlib import ExitStack

import concourse.mybir as mybir
from concourse.masks import make_identity

K, H, T, S, T2 = 1536, 1024, 2048, 512, 1024
FLOPS = 5100273664

F32 = mybir.dt.float32
BF16 = mybir.dt.bfloat16
I32 = mybir.dt.int32
U32 = mybir.dt.uint32
U16 = mybir.dt.uint16
U8 = mybir.dt.uint8
FP8X4 = mybir.dt.float8_e4m3fn_x4
FP4X4 = mybir.dt.float4_e2m1fn_x4
ALU = mybir.AluOpType
ACT = mybir.ActivationFunctionType

P = 128
PACK = 4
KP = P * PACK
NA = K // KP
NB = H // KP
NM = S // P
QUADS = 4
RUN = 4
ALIGN = 64

PLACE = {
    "h0": 1, "h1": 0, "h2": 2, "h3": 3, "h4": 2, "h5": 4, "h6": 2, "h7": 4,
    "v2w0": 2, "v2s": 4, "v2w1": 4.5,
    "act0": 11, "act1": 5, "w1q10g": 8, "w1q11g": 12, "w1q12xg": 6, "w1q12yg": 4,
    "w3q0g": 8, "w3q1g": 12, "w3q2g": 24,
    "w1q00g": 16, "w1q01g": 20, "w1q02xg": 18, "w1q02yg": 22, "vw0": 28, "vw1": 16, "vw2": 18,
    "tabs": 30, "w2w0": 36, "w2w1": 39, "w2s": 42, "flat1": 30,
    "w1r12": 46, "flat0": 46,
    "wgs_rows": 24, "spread": 54, "tab2s": 62,
    "w1r00": 94, "wgs0": 94, "wgs1": 96, "wgs2": 98, "wgs3": 100,
    "tabw0": 64, "tabw1": 72, "tabw2": 80, "tab2w0": 64, "tab2w1": 72,
    "w2d1": 80, "w2sd1": 84, "w2d0": 88, "w2sd0": 91,
}


def tile_list_ore_ejection_scores_kernel(
    tc, tab_words, tab_scales, tab2_words, tab2_scales, w1, w2_words, w2_scales, w3,
    gain, page0, wgs, trail, offs, offs2, offs3, pos1, pos2, out,
):
    nc = tc.nc
    with ExitStack() as ctx:
        lists = ctx.enter_context(tc.tile_pool(name="lists", bufs=1))
        sb = ctx.enter_context(tc.tile_pool(name="sb", bufs=1))
        hp = ctx.enter_context(tc.tile_pool(name="hp", bufs=1))
        ps = ctx.enter_context(tc.psum_pool(name="ps", bufs=1))

        def sbuf(name, shape, dtype, tag=None, bufs=1):
            if name in PLACE:
                offset = int(PLACE[name] * 1024)
                return hp.tile(shape, dtype, name=name, tag=name, align_bytes=ALIGN, offset=offset)
            return sb.tile(shape, dtype, name=name, tag=tag or name, bufs=bufs, align_bytes=ALIGN)

        def bank(name, shape, tag):
            return ps.tile(shape, F32, name=name, tag=tag, bufs={"a1": 3, "lin": 2, "e": 3}[tag])

        def load_list(name, dram):
            offsets = lists.tile([P, S // 16], U16, name=name)
            nc.sync.dma_start(offsets[:], dram)
            return offsets

        def zeroed_scale_tile(name, width):
            rows = sbuf(name, [P, width], U8)
            nc.vector.memset(rows[:].bitcast(I32), 0)
            return rows

        def load_scale_rows(rows, dram):
            src = dram.rearrange("a (q r) c -> r q a c", r=4)
            for r in range(4):
                nc.sync.dma_start(
                    out=rows[r:P:32, :].bitcast(I32).rearrange("q (a w) -> q a w", a=NA),
                    in_=src[r].bitcast(I32),
                )

        def load_words(name, dram_pass):
            words = sbuf(name, [P, T], I32)
            nc.sync.dma_start(out=words[:], in_=dram_pass.rearrange("p t i -> p (t i)").bitcast(I32))
            return words

        def load_raw(name, w, a, c0):
            raw = sbuf(name, [P, PACK, KP], F32, tag="raw", bufs=NA)
            nc.sync.dma_start(
                out=raw[:], in_=w[a * KP:(a + 1) * KP, c0:c0 + KP].rearrange("(p j) c -> p j c", j=PACK)
            )
            return raw

        def load_page(s):
            b, t = divmod(s, PACK)
            page = sbuf("page%d" % s, [P, T2], F32)
            rows = page0[b * KP:(b + 1) * KP, :].rearrange("(p t) n -> t p n", t=PACK)
            nc.sync.dma_start(out=page[:], in_=rows[t])
            return page

        def deal_wgs(rows):
            ident = sbuf("ident", [P, P], F32)
            make_identity(nc, ident[:])
            turned = bank("turned", [P, PACK, P], "e")
            for c in range(PACK):
                nc.tensor.transpose(turned[:, c, :], rows[:, c * P:(c + 1) * P], ident[:])
            spread = sbuf("spread", [P, PACK, PACK, QUADS, 32], F32)
            for c in range(PACK):
                src = turned[:, c, :].rearrange("p (q t) -> p t q", t=PACK).unsqueeze(2)
                nc.scalar.copy(out=spread[:, c], in_=src.to_broadcast([P, PACK, QUADS, 32]))
            dealt = []
            for t in range(PACK):
                returned = bank("wgsb%d" % t, [P, S], "e")
                for c in range(PACK):
                    nc.tensor.transpose(
                        returned[:, c * P:(c + 1) * P], spread[:, c, t].rearrange("p u q -> p (u q)"), ident[:]
                    )
                weights = sbuf("wgs%d" % t, [P, S], F32)
                nc.scalar.copy(out=weights[:], in_=returned[:])
                dealt.append(weights[:])
            return dealt

        def gather(dst, window, offsets):
            nc.vector.tensor_copy(dst, window.indirect(offsets[:]))

        def quantise(name, grouped, width):
            codes = sbuf(name + "c", [P, width], U32)
            scales = sbuf(name + "s", [P, width], U8)
            nc.vector.quantize_mx(out=codes[:].bitcast(FP8X4), scales=scales[:], in_=grouped)
            return codes, scales

        def quantise_w1(name, raw, t0, nt):
            grouped = sbuf(name + "g", [P, nt * P * PACK], BF16)
            nc.scalar.copy(
                out=grouped[:].rearrange("p (t m j) -> p m t j", t=nt, j=PACK),
                in_=raw[:].rearrange("p j (m t) -> p m t j", t=PACK)[:, :, t0:t0 + nt, :],
            )
            codes, scales = quantise(name, grouped[:], nt * P)
            return [(codes[:, i * P:(i + 1) * P], scales[:, i * P:(i + 1) * P]) for i in range(nt)]

        def quantise_w3(name, raw):
            grouped = sbuf(name + "g", [P, KP * PACK], BF16)
            nc.scalar.copy(
                out=grouped[:].rearrange("p (c i j) -> p c j i", i=RUN, j=PACK),
                in_=raw[:].rearrange("p j (c i) -> p c j i", i=RUN),
            )
            return quantise(name, grouped[:], KP)

        def mx(acc, lhs, lhs_scale, rhs, rhs_scale, first, last, lhs_dtype=FP8X4):
            nc.tensor.matmul_mx(
                out=acc, lhsT=lhs.bitcast(lhs_dtype), lhsT_scale=lhs_scale,
                rhs=rhs.bitcast(FP8X4), rhs_scale=rhs_scale, start=first, stop=last,
            )

        tabs = zeroed_scale_tile("tabs", NA * T)
        w2s = zeroed_scale_tile("w2s", NA * H)
        tab2s = zeroed_scale_tile("tab2s", T)
        warm_in = sbuf("warm_in", [P, 1], F32)
        nc.gpsimd.memset(warm_in[:], 0.0)
        warm_out = sbuf("warm_out", [P, 1], F32)
        nc.scalar.activation(out=warm_out[:], in_=warm_in[:], func=ACT.Gelu_apprx_tanh)

        vw, vs = [], []
        w1q = {}
        w2d, w2sd = {}, {}

        def deal(name, src, dtype):
            dst = sbuf(name, [P, NA * KP], dtype)
            nc.vector.tensor_copy(dst[:].rearrange("p (a t m) -> p t a m", a=NA, t=PACK), src)
            return dst

        def w2_words_half(b):
            words = sbuf("w2w%d" % b, [P, NA * KP], U16)
            nc.sync.dma_start(
                out=words[:].bitcast(I32).rearrange("p (a w) -> p a w", a=NA),
                in_=w2_words[:, :, 2 * b * KP:2 * (b + 1) * KP].rearrange("a p c -> p a c").bitcast(I32),
            )
            w2d[b] = deal("w2d%d" % b, words[:].rearrange("p (a m t) -> p t a m", a=NA, t=PACK), U16)

        def w2_scales_half(b):
            half = w2s[:].rearrange("p (a b m t) -> p b t a m", a=NA, b=NB, t=PACK)[:, b]
            w2sd[b] = deal("w2sd%d" % b, half, U8)

        def gather_tab(a, words):
            picked = sbuf("vw%d" % a, [P, S], U32)
            gather(picked[:], words[:].bitcast(U32), offs_t)
            vw.append(picked)
            picked_scales = sbuf("vs%d" % a, [P, S], U8)
            gather(picked_scales[:], tabs[:, a * T:(a + 1) * T], offs_t)
            vs.append(picked_scales)

        words0 = load_words("tabw0", tab_words[0])
        offs_t = load_list("offs", offs)
        wgs_rows = sbuf("wgs_rows", [P, S], F32)
        nc.sync.dma_start(out=wgs_rows[:], in_=wgs)
        raw0 = load_raw("w1r00", w1, 0, 0)
        w2_words_half(0)
        load_scale_rows(tabs, tab_scales)
        gather_tab(0, words0)
        w1q[0, 0] = quantise_w1("w1q00", raw0, 0, PACK)
        wgs_t = deal_wgs(wgs_rows)
        words1 = load_words("tabw1", tab_words[1])
        raw1 = load_raw("w1r01", w1, 1, 0)
        load_scale_rows(w2s, w2_scales)
        w2_scales_half(0)
        gather_tab(1, words1)
        w1q[0, 1] = quantise_w1("w1q01", raw1, 0, PACK)
        raw2 = load_raw("w1r02", w1, 2, 0)
        words2 = load_words("tabw2", tab_words[2])
        w1q[0, 2] = quantise_w1("w1q02x", raw2, 0, 2)
        gather_tab(2, words2)
        w1q[0, 2] += quantise_w1("w1q02y", raw2, 2, 2)
        gain_t = sbuf("gain", [P, NB * PACK], F32)
        nc.sync.dma_start(
            out=gain_t[:].rearrange("p (b t) -> p b t", t=PACK),
            in_=gain.rearrange("(b p t) -> p b t", b=NB, t=PACK),
        )
        w2_scales_half(1)
        w2_words_half(1)

        pages = {}

        def feature_slice(s):
            b, t = divmod(s, PACK)
            a1 = bank("a1_%d" % s, [P, S], "a1")
            for a in range(NA):
                codes, scales = w1q[b, a][t]
                mx(a1[:], codes, scales, vw[a][:], vs[a][:], a == 0, a == NA - 1)
            lin = bank("lin_%d" % s, [P, S], "lin")
            for a in range(NA):
                cols = slice(a * KP + t * P, a * KP + (t + 1) * P)
                mx(lin[:], w2d[b][:, cols], w2sd[b][:, cols], vw[a][:], vs[a][:], a == 0, a == NA - 1, FP4X4)
            act = sbuf("act%d" % s, [P, S], F32, tag="act", bufs=3)
            nc.scalar.activation(out=act[:], in_=a1[:], func=ACT.Gelu_apprx_tanh)
            h = sbuf("h%d" % s, [P, S], F32)
            nc.vector.scalar_tensor_tensor(
                out=h[:], in0=act[:], scalar=gain_t[:, s:s + 1], in1=lin[:], op0=ALU.mult, op1=ALU.add
            )
            nc.vector.tensor_tensor(pages[s][:].indirect(offs3_t[:]), h[:], wgs_t[t], ALU.mult)

        offs3_t = load_list("offs3", offs3)
        pages[0] = load_page(0)
        raws = []
        for a in range(NA):
            raws.append(load_raw("w1r1%d" % a, w1, a, KP))
            pages[a + 1] = load_page(a + 1)
        feature_slice(0)
        w1q[1, 0] = quantise_w1("w1q10", raws[0], 0, PACK)
        feature_slice(1)
        w1q[1, 1] = quantise_w1("w1q11", raws[1], 0, PACK)
        feature_slice(2)
        w1q[1, 2] = quantise_w1("w1q12x", raws[2], 0, 2) + quantise_w1("w1q12y", raws[2], 2, 2)
        feature_slice(3)

        w3r = []
        pages[4] = load_page(4)
        w3r.append(load_raw("w3r0", w3, 0, 0))
        pages[5] = load_page(5)
        pages[6] = load_page(6)
        w3r.append(load_raw("w3r1", w3, 1, 0))
        pages[7] = load_page(7)
        w3r.append(load_raw("w3r2", w3, 2, 0))
        offs2_t = load_list("offs2", offs2)
        tab2w = [load_words("tab2w%d" % b, tab2_words[b]) for b in range(NB)]
        for q in range(QUADS):
            nc.sync.dma_start(
                out=tab2s[32 * q:32 * q + 4 * NB, :].bitcast(I32),
                in_=tab2_scales[:, 4 * q:4 * q + 4, :].bitcast(I32),
            )
        pos1_t = load_list("pos1", pos1)
        pos2_t = load_list("pos2", pos2)
        trail_t = sbuf("trail", [P, NM], F32)
        with nc.allow_non_contiguous_dma(reason="one value a partition"):
            nc.sync.dma_start(out=trail_t[:], in_=trail.rearrange("(c p) -> p c", p=P))

        def round_page(flat, s, cols):
            nc.scalar.copy(out=flat[:, s % PACK, cols], in_=pages[s][:, cols])

        def weave_and_quantise(b, i, flat):
            grouped = sbuf("pg%d%d" % (b, i), [P, S * PACK], BF16)
            nc.scalar.copy(
                out=grouped[:].rearrange("p (c i t) -> p c t i", i=RUN, t=PACK),
                in_=flat[:, :, halves[i]].rearrange("p t (c i) -> p c t i", i=RUN),
            )
            return quantise("pq%d%d" % (b, i), grouped[:], S)

        whole = slice(0, T2)
        halves = [slice(0, S), slice(S, T2)]
        feature_slice(4)
        feature_slice(5)
        feature_slice(6)
        flat0 = sbuf("flat0", [P, PACK, T2], BF16)
        for s in range(PACK):
            round_page(flat0, s, whole)
        feature_slice(7)
        w3q = [quantise_w3("w3q0", w3r[0])]
        pq0 = [weave_and_quantise(0, i, flat0) for i in range(len(halves))]
        w3q.append(quantise_w3("w3q1", w3r[1]))
        w3q.append(quantise_w3("w3q2", w3r[2]))
        flat1 = sbuf("flat1", [P, PACK, T2], BF16)
        last = NB * PACK - 1
        for s in range(PACK, last):
            round_page(flat1, s, whole)

        v2s = sbuf("v2s", [P, S], U8)
        gather(v2s[:], tab2s[:], offs2_t)
        v2w = [sbuf("v2w%d" % b, [P, S], U32) for b in range(NB)]
        for b in range(NB):
            gather(v2w[b][:], tab2w[b][:].bitcast(U32), offs2_t)
        pq1 = []
        for i, half in enumerate(halves):
            round_page(flat1, last, half)
            pq1.append(weave_and_quantise(1, i, flat1))

        for m in range(NM):
            rows = slice(m * P, (m + 1) * P)
            e = sbuf("e%d" % m, [P, T2], F32, tag="raw", bufs=NA)
            for i, half in enumerate(halves):
                acc = bank("e%d_%d" % (m, i), [P, S], "e")
                mx(acc[:], v2w[0][:, rows], v2s[:, rows], pq0[i][0][:], pq0[i][1][:], True, False)
                mx(acc[:], v2w[1][:, rows], v2s[4:P, rows], pq1[i][0][:], pq1[i][1][:], False, True)
                nc.scalar.copy(out=e[:, half], in_=acc[:])
            acc = bank("d%d" % m, [P, S], "lin")
            for a in range(NA):
                mx(acc[:], w3q[a][0][:, rows], w3q[a][1][:, rows], vw[a][:], vs[a][:], a == 0, a == NA - 1)
            direct = sbuf("direct%d" % m, [P, S], F32, tag="direct", bufs=2)
            nc.scalar.copy(out=direct[:], in_=acc[:])
            back = sbuf("back%d" % m, [P, S], F32, tag="act", bufs=3)
            gather(back[:], e[:], pos2_t)
            lead = sbuf("lead%d" % m, [P, S], F32, tag="lead", bufs=2)
            nc.vector.tensor_tensor(lead[:], e[:].indirect(pos1_t[:]), direct[:], ALU.add)
            res = sbuf("res%d" % m, [P, S], F32, tag="res", bufs=2)
            nc.vector.scalar_tensor_tensor(
                out=res[:], in0=back[:], scalar=trail_t[:, m:m + 1], in1=lead[:], op0=ALU.mult, op1=ALU.max
            )
            nc.sync.dma_start(out=out[rows, :], in_=res[:])
